import numpy as np, ml_dtypes
CORES = [40,41,42,43,44,45,46,47]
N = 8
import mx_ref
BF = ml_dtypes.bfloat16
def gentries(a):
    return np.ascontiguousarray(a.reshape(8, 16, -1).transpose(0, 2, 1)).reshape(8, -1)
def gtable(e):
    e = np.asarray(e); return np.ascontiguousarray(e.reshape(8, -1, 16).transpose(0, 2, 1)).reshape(128, -1).astype(np.int32)
def gcols(t, e):
    v = np.concatenate([t.reshape(8, 16, -1, 4), np.zeros((8, 16, 1, 4), BF)], axis=2)
    return np.ascontiguousarray(np.stack([v[g][:, e[g]] for g in range(8)])).reshape(128, -1)
def gpick(z, e):
    return np.concatenate([z[16 * g:16 * g + 16][:, e[g]] for g in range(8)])
def tile(rs):
    return np.stack(rs, axis=2).reshape(128, -1).astype(BF)
def pick(q, e):
    c = np.concatenate([q[0].reshape(128, -1, 4), np.zeros((128, 1, 4), np.uint8)], axis=1); s = np.concatenate([q[1], np.ones((16, 1), np.uint8)], axis=1)
    return (np.ascontiguousarray(c[:, e].reshape(128, -1)), np.ascontiguousarray(s[:, e]))
def join(*qs):
    return (np.concatenate([q[0] for q in qs], axis=1), np.concatenate([q[1] for q in qs], axis=1))
def put(q, e, v):
    c, s = q[0].reshape(128, -1, 4).copy(), q[1].copy(); c[:, e] = v[0].reshape(128, -1, 4); s[:, e] = v[1]
    return (c.reshape(128, -1), s)
def pk(c, s):
    return (np.ascontiguousarray(c), mx_ref.live(s))
def emit(q):
    return q[0], q[1]
def packed(v, rng):
    q = [mx_ref.quantize(np.ascontiguousarray(v[r])) for r in range(N)]
    return np.stack([a for a, b in q]), np.stack([mx_ref.plane(b, rng) for a, b in q])
def values_of_codes():
    e, c = np.zeros((128, 128, 4), np.float32), np.zeros((128, 2, 4), np.uint8)
    e[np.arange(128), np.arange(128), 0] = 1
    c[:127, :, 0] = np.arange(256).reshape(2, 128).T[:127]
    return mx_ref.matmul(mx_ref.quantize(e.reshape(128, 512).astype(BF)), (c.reshape(128, 8), np.full((16, 2), 127, np.uint8))).T.reshape(-1).astype(np.float64)
CODE_VALUE, SCALE_VALUE = values_of_codes(), 2.0 ** (np.arange(256) - 127.0)
def decode(q):
    return (CODE_VALUE[q[0]].reshape(16, 8, -1, 4) * SCALE_VALUE[q[1]][:, None, :, None] + 0.0).reshape(128, -1).astype(np.float32)
def f(rng, *shape):
    return mx_ref.flush((rng.standard_normal(shape, dtype=np.float32) * np.exp2(rng.integers(-2, 3, shape[:-1] + (1,)))).astype(BF))
def wide(rng, *shape, cols=0):
    v = rng.standard_normal(shape, dtype=np.float32) * np.exp2(rng.integers(-12, 13, shape)).astype(np.float32)
    if cols: v *= np.repeat(np.exp2(rng.integers(-cols, cols + 1, shape[:-2] + (1, shape[-1] // 4))) * (rng.random(shape[:-2] + (1, shape[-1] // 4)) > 0.0625), 4, axis=-1).astype(np.float32)
    return mx_ref.flush(v.astype(BF))
C, K, P, R = 384, 96, 192, 3
def numbers_of(rng):
    return {"x": np.array(f(rng, N, 128, 4 * C)), "u": np.array(f(rng, N, 128, 512)), "v": np.array(f(rng, N, 128, 512))}
def mixed(rng):
    return rng.permuted(np.tile(np.arange(C), (N, 8, 1)), axis=2)
def links(e):
    return np.stack([gtable(e[r]) for r in range(N)])
def packedw(rng, w):
    c, p = packed(np.ascontiguousarray(w).reshape(N, 128, 2048), rng)
    return {"wc": c, "ws": p}
def weights(rng, still=()):
    w = np.array(f(rng, N, 128, 2048)).reshape(N, 8, 16, 4, 8, 16, 4)
    for i in still:
        w[:, :, i] = 0
        w[:, :, :, :, :, i] = 0
    return packedw(rng, w)
def setup_inputs(rng):
    return {**numbers_of(rng), "link": links(mixed(rng)), **weights(rng)}
def setup_inputs_ties(rng):
    d = numbers_of(rng)
    e = rng.permutation(N)
    x = d["x"].reshape(N, 8, 16, C, 4)
    for r in range(N):
        k = rng.permutation(C) % 3
        if r == e[0]: k = np.zeros(C, int)
        elif r in e[2::2]: k = rng.permutation(3)[np.arange(C) % 3]
        a = x[r][:, :8, :3].copy()
        a[:, :, 2] = 0
        x[r][:, :8] = a[:, :, k]
    x[e[1]] = 0
    u = d["u"].reshape(N, 8, 16, 128, 4)
    u[:, :, 8:, ::16] = 0
    u[:, :, 8:, 1::16] = 0
    t = mixed(rng)
    t[e[2]] = np.arange(C)
    t[e[3]] = t[e[3], :1].copy()
    return {"x": x.reshape(N, 128, 4 * C), "u": u.reshape(N, 128, 512), "v": d["v"], "link": links(t), **weights(rng, range(8))}
def setup_inputs_near(rng):
    d = numbers_of(rng)
    x = d["x"].astype(np.float32).reshape(N, 8, 16, C, 4)
    x[:, :, 0] = 0
    x[:, :, 8:] = 0
    u = d["u"].reshape(N, 128, 128, 4)
    u[:, :, ::16] = 0
    u[:, :, 1::16] = 0
    o = rng.permutation(N) % 4
    s = rng.integers(0, 256, (N, 8, C))
    for r in range(N):
        low = 2.0 ** -29 if o[r] == 3 else 2.0 ** -23
        for i in range(2): x[r, :, 8 + i] = ((s[r][:, :, None] >> (4 * i + np.arange(4))) & 1) * np.exp2(4.0 * i + np.arange(4)) * low
        x[r, :, 12, :, 0] = rng.integers(-1, 2, (8, C)) * (2.0 ** -29 if o[r] == 3 else 2.0 ** -20)
        if o[r] == 3: x[r, :, 13, :, 0] = x[r, :, 12, :, 0]
        if o[r] < 2:
            x[r, :, 0, :, 0] = rng.integers(0, 2, (8, C)) * 2.0 - 1.0
            x[r, :, 11, :, 0] = 2.0 ** -10
        if o[r] == 2:
            for g in range(8): x[r, g, 0, rng.permutation(C)[:2], 0] = np.array([1.0, -1.0])
        for g in rng.permutation(8)[:4]: x[r, g, 12, rng.integers(C), 0] = 2.0 ** 29 * rng.choice([-1.0, 1.0])
        k = 1.0 if o[r] == 0 else 2.0 ** -30
        for h in range(0, 128, 16):
            if o[r] < 2:
                u[r, h, h, 0] = k
                u[r, h + 11, h, 0] = k
            if o[r] == 2: u[r, h, h, 0] = 1.0
            u[r, h + 8, h] = k
            u[r, h + 9, h] = k
            u[r, h + 12, h + 1, 0] = 1.125 * 2.0 ** -30 if o[r] == 3 else 2.0 ** -30
            if o[r] == 3: u[r, h + 13, h + 1, 0] = -1.0 * 2.0 ** -30
    return {"x": x.reshape(N, 128, 4 * C).astype(BF), "u": u.reshape(N, 128, 512), "v": d["v"], "link": links(mixed(rng)), **weights(rng, [0, 8, 9, 10, 11, 12, 13, 14, 15])}
def setup_inputs_caps(rng):
    d = numbers_of(rng)
    x = np.zeros((N, 8, 16, C, 4))
    z = (N, 8, 8, C, 4)
    x[:, :, :8] = rng.choice([-1.0, 1.0], z) * (1.0 + (2 * rng.integers(0, 64, z) + 1) * 2.0 ** -7) * np.exp2(-1.0 * rng.integers(8, 15, z))
    x[:, :, 0, :, 0] = rng.choice([1.96875, 1.84375], (N, 8, C))
    s = mixed(rng)
    for i in range(3): x[:, :, 8 + i] = ((s[:, :, :, None] >> (4 * i + np.arange(4))) & 1) * np.exp2(4.0 * i + np.arange(4))
    side = rng.permutation(N) % 2 * 2 - 1
    q = np.argsort(-s * side[:, None, None], axis=2)[:, :, 1::2]
    one = rng.random((N, 8, C)) < 0.5
    a = rng.permutation(8)
    for i in range(6):
        g, t, k = a[i], i % R, 0
        for r in range(N):
            if (r >> t) & 1: one[r, g] = True
            else:
                n = K if i < 3 else K - 1 + 2 * (k % 2)
                k += 1
                one[r, g, q[r, g]] = rng.permutation(P) < n
    one[:, a[6]] = (((np.arange(N) >> (R - 1)) & 1) == 1)[:, None]
    one[:, a[7]] = ((np.arange(N) & 1) == 1)[:, None]
    x[:, :, 12, :, 0] = np.where(one, 1.0, -1.0 * rng.integers(0, 2, (N, 8, C)))
    u = d["u"].reshape(N, 128, 128, 4)
    u[:, :, ::16] = 0
    u[:, :, 1::16] = 0
    for r in range(N):
        for h in range(0, 128, 16):
            u[r, h + 8:h + 11, h] = float(side[r])
            u[r, h + 12, h + 1, 0] = 1.0
    return {"x": x.astype(np.float32).reshape(N, 128, 4 * C).astype(BF), "u": u.reshape(N, 128, 512), "v": d["v"], "link": links(mixed(rng)), **weights(rng, range(8, 16))}
def setup_inputs_huge(rng):
    d = numbers_of(rng)
    o = rng.permutation(N)
    c = rng.integers(0, 2, (N, 1, 1, C, 1)) * 2.0 - 1.0
    c[:, :, :, :2] = np.array([1.0, -1.0])[:, None]
    c[o == 1] = -1.0
    c[o == 2] = 1.0
    x = 0.6 + 0.09 * rng.random((N, 8, 16, C, 4))
    x[o == 0] = np.where(rng.random((1, 8, 16, C, 4)) < 0.125, 0.8125, 0.875)
    u = d["u"].reshape(N, 128, 128, 4)
    for i in range(2):
        a = 2.0 ** 29 * (1.0 - 0.1 * rng.random((N, 128, 8, 4)))
        a[o == 0] = 2.0 ** 30 * np.where(rng.random((1, 128, 8, 4)) < 0.03125, 0.875, 1.0)
        turned = (o % 2 == 1) if i else (o == 0) | (o > N // 2)
        for r in range(N):
            if turned[r]: a[r] *= (rng.permutation(8) % 2 * 2.0 - 1.0)[None, :, None]
        u[:, :, i::16] = a.astype(np.float32).astype(BF)
    w = np.zeros((N, 128, 4, 128, 4), np.float32)
    i = np.arange(128)
    for b in range(4): w[:, i, b, i, b] = 1
    return {"x": (2.0 ** 30 * x * c).astype(np.float32).reshape(N, 128, 4 * C).astype(BF), "u": u.reshape(N, 128, 512), "v": d["v"], "link": links(mixed(rng)), **packedw(rng, w.astype(BF))}
def setup_inputs_spread(rng):
    d = setup_inputs(rng)
    d["x"] = wide(rng, N, 128, 4 * C, cols=6)
    return d
def check_inputs(d):
    b = []
    for k in ("x", "u", "v"):
        a = np.abs(d[k].astype(np.float32))
        if not (np.isfinite(a).all() and ((a == 0) | (a >= 2.0 ** -30) & (a <= 2.0 ** 30)).all()): b.append("a value of " + k)
    none, least, most = [emit(mx_ref.quantize(np.full((128, 16), k, np.float32).astype(BF)))[1][0, 0] for k in (0.0, 2.0 ** -30, 2.0 ** 30)]
    for r in range(N):
        if (np.sort(gentries(d["link"][r]), axis=1) != np.arange(C)).any(): b.append("link: a group's entries are no permutation")
        if ((d["wc"][r] == 0x7F) | (d["wc"][r] == 0xFF)).any(): b.append("wc: a code that is no number")
        s = mx_ref.live(d["ws"][r])
        if ((s != none) & ((s < least) | (s > most))).any(): b.append("ws: a scale out of range")
    return b
def at(a, e):
    return np.take_along_axis(a, e, axis=1)
def reference(x, u, v, link, wc, ws):
    qu = [mx_ref.quantize(u[r]) for r in range(N)]
    lay = [pk(wc[r], ws[r]) for r in range(N)]
    now = [x[r] for r in range(N)]
    to = [gentries(link[r]) for r in range(N)]
    for t in range(R):
        d = 2 ** t
        own, order, bit = [], [], []
        for r in range(N):
            q = mx_ref.quantize(now[r])
            own.append(decode(q))
            s = mx_ref.matmul(qu[r], q)
            order.append(np.argsort(-(s[::16] + np.float32(0.0)), axis=1, kind="stable"))
            bit.append(s[1::16] > 0)
        kept, names, left, places, turned = [], [], [], [], []
        for r in range(N):
            k, q = order[r][:, 0::2], order[r][:, 1::2]
            there = at(to[r], q)
            fails = at(bit[r], q) != at(bit[(r + d) % N], there)
            j = np.argsort(fails.astype(np.int64), axis=1, kind="stable")
            k, q, there = at(k, j), at(q, j), at(there, j)
            h = own[r].astype(BF)
            a = ((gcols(h, k).astype(np.float32) + gcols(h, q).astype(np.float32)) * np.float32(0.5)).astype(BF)
            kept.append(mx_ref.quantize(np.ascontiguousarray(a[:, :4 * K])))
            left.append(mx_ref.quantize(np.ascontiguousarray(a[:, 4 * K:])))
            names.append(there[:, :K])
            places.append(q[:, K:])
            m = np.tile(np.arange(C), (8, 1))
            np.put_along_axis(m, k[:, K:], q[:, K:], axis=1)
            np.put_along_axis(m, q[:, K:], k[:, K:], axis=1)
            turned.append(at(to[r], m))
        to = [at(turned[(r + d) % N], to[r]) for r in range(N)]
        for r in range(N):
            c = (r - d) % N
            slots = join(kept[c], left[r])
            e = np.full((8, C), P)
            np.put_along_axis(e, places[r], np.tile(np.arange(K, P), (8, 1)), axis=1)
            np.put_along_axis(e, names[c], np.tile(np.arange(K), (8, 1)), axis=1)
            made = []
            for b in range(4):
                h = mx_ref.matmul(pick(lay[r], np.arange(128 * b, 128 * b + 128)), slots)
                h = np.concatenate([h, np.zeros((128, 1), np.float32)], axis=1)
                made.append(gpick(h, e) * np.float32(0.03125) + own[r][:, b::4])
            now[r] = tile(made)
    y, lk = np.zeros((N, 128, C), np.float32), np.zeros((N, 8, C), np.float32)
    oc, osc = np.zeros((N, 128, 4 * C), np.uint8), np.zeros((N, 16, C), np.uint8)
    for r in range(N):
        q = mx_ref.quantize(now[r])
        y[r] = mx_ref.matmul(mx_ref.quantize(v[r]), q)
        lk[r] = to[r]
        oc[r], osc[r] = emit(q)
    return {"y": y, "lk": lk, "oc": oc, "osc": osc}

@@ -1,0 +1,414 @@
+from concourse.mybir import dt, AluOpType, ActivationFunctionType
+
+AL, AF = AluOpType, ActivationFunctionType
+NR = 3
+BIG = 1.0e29
+BV = float(2 ** 19)
+TILES = [("fa", [23, 22, 21], 384), ("fb", [20, 19, 18, 17], 320), ("fc", [16, 15, 14, 13], 256),
+         ("fd", [12, 11, 10, 9], 192), ("fe", [8, 7, 6, 5], 128), ("ff", [4, 3, 2, 1], 128)]
+
+SCRATCH, WHERE = {}, {}
+
+
+def _s(names, dtype, where="sbuf", buf=None):
+    buf, n = buf or names[0][0], 0
+    for name, w in names:
+        WHERE[name] = (buf, n, w)
+        if dtype == "codes":
+            WHERE[name + "s"] = (buf + "s", n, w)
+        n += w
+    SCRATCH[buf] = (where, [128, n], "float8_e4m3fn_x4" if dtype == "codes" else dtype)
+    if dtype == "codes":
+        SCRATCH[buf + "s"] = (where, [128, n], "uint8")
+
+
+def _each(text, dtype):
+    for w in text.split():
+        n, c = w.split(":")
+        _s([(n, int(c))], dtype)
+
+
+_each("xt0:1536 xt1:1536 xt2:1536 xt3:1536 fh:1536 ut:512 vt:512 iet:2048 bot:512 zt:512 ak:512 al:512 one:512 sg:384 bt:384 rds:384 "
+      "r0:384 tb:384 w2:768 fl:192 flc:192 junk:4416 rl:384 ra:384", "bfloat16")
+_s([("r0w", 16), ("tbw", 16), ("cw", 16)], "bfloat16", buf="kb")
+_s([(_n, 4 * _w) for _n, _l, _w in TILES], "bfloat16", buf="ft")
+_s([("q" + _n, _w) for _n, _l, _w in TILES], "codes", buf="qf")
+_each("xq:384 uq:128 urs:128 urb:128 vq:128 eq:512 bo:128 wq:512 ql:128", "codes")
+for _t in "012":
+    _each("qk%s:128 vb%s:128" % (_t, _t), "codes")
+    _each(" ".join(_n + _t + ":24" for _n in ("sb", "lb", "sn", "ln", "st", "lt")), "uint16")
+_s([(_n, 16) for _n in ("ks", "ks4", "mbw", "rsw", "t16w", "t4w", "ta", "tn", "cols")], "float32", buf="kw")
+_s([("c4", 192), ("c16", 192), ("fc2", 192), ("fcum", 192)], "float32", buf="cc")
+_s([("kq", 192), ("lqk", 96), ("nmc", 96)], "float32", buf="kn")
+_s([("mc", 384), ("tuc", 384), ("lc", 384)], "float32", buf="sc3")
+_each("kj:36 iota0:384 iota1:384 mb:384 rs:384 t16:384 t4:192 m2:384 hs:384 ru:24 kr:72 ow:72 pay:384 sp:384 kaqa:384 kqs:192 pp:60 "
+      "fq:768 fl32:384 fn32:384 sl:384 sa:384 val:192 tu:384 tr:384 lr0:384 lr1:384 lr2:384 lr3:384 ys:384", "float32")
+_each("li:24 pi:12 kqi:180", "int32")
+_each("pmo:24 uo16:16 lt16:24 off16:24 rk16:24 n16:12 t4q:48 t4k:48 tqk:6 tll:12", "uint16")
+_s([("p%d" % _b, 512) for _b in range(8)], "float32", "psum", "ps")
+
+SEMAPHORES = "v a p gc ls dx du dw ds dv dl oy ok oc_ o0 o1 o2 o3 rb0 rb1 rb2 rn0 rn1 rn2 rc0 rc1 rc2 rt0 rt1 rt2".split()
+
+
+def R(name, lo=0, hi=None, step=1, bit=None):
+    buf, at, w = WHERE[name]
+    return (buf, at + lo, at + (w if hi is None else hi), step, bit)
+
+
+def IND(win, off):
+    return ("ind", win, off)
+
+
+def flat(rs):
+    return [x for r in rs for x in (r[1:] if r[0] == "ind" else (r,))]
+
+
+def meets(x, y):
+    if x[1] <= y[0] or y[1] <= x[0]:
+        return False
+    return not (x[2] == y[2] and x[2] > 1 and (x[0] - y[0]) % x[2])
+
+
+def rank_program(g, core, T, topo):
+    rank = T.rank_of(core)
+    if rank is None:
+        return
+    ENG = {"v": g.vector, "a": g.scalar, "p": g.tensor, "g": g, "s": g.sync}
+    CNT = {"v": 0, "a": 0, "p": 0, "gc": 0, "ls": 0}
+    know = {q: {} for q in ENG}
+    clocks, writes, reads, seq = {}, {}, {}, [0]
+
+    def ap(r):
+        if r[0] == "ind":
+            return ap(r[1]).indirect(ap(r[2]))
+        n, lo, hi, st, bit = r
+        w = T[n][:, lo:hi] if st == 1 else T[n][:, lo:hi:st]
+        return w if bit is None else w.bitcast(dt.uint8 if bit == "u8" else dt.uint32)
+
+    def hold(q, rd, wr, loose=False):
+        need = {}
+        for r in flat(rd):
+            for x, ev, own in writes.get(r[0], []):
+                if meets(x, r[1:4]):
+                    need[ev] = 1
+        for r in flat(wr):
+            for x, ev, own in writes.get(r[0], []) + reads.get(r[0], []):
+                if meets(x, r[1:4]) and not (loose and own == q):
+                    need[ev] = 1
+        for ev in sorted(need, key=lambda e: -clocks[e]["#"]):
+            if know[q].get(ev[0], 0) < ev[1]:
+                ENG[q].wait_ge(T.sem[ev[0]], ev[1])
+                for k, n in clocks[ev].items():
+                    if know[q].get(k, 0) < n:
+                        know[q][k] = n
+
+    def done(q, rd, wr, ev):
+        c = dict(know[q])
+        seq[0] += 1
+        c.update({ev[0]: max(c.get(ev[0], 0), ev[1]), "#": seq[0]})
+        clocks[ev] = c
+        for r in flat(rd):
+            reads.setdefault(r[0], []).append((r[1:4], ev, q))
+        for r in flat(wr):
+            x = r[1:4]
+            if x[2] == 1:
+                for d in (writes, reads):
+                    d[r[0]] = [e for e in d.get(r[0], []) if not (x[0] <= e[0][0] and e[0][1] <= x[1])]
+            writes.setdefault(r[0], []).append((x, ev, q))
+
+    def op(q, rd, wr, call, loose=False):
+        hold(q, rd, wr, loose)
+        sem = "gc" if q == "g" else q
+        CNT[sem] += 1
+        call().then_inc(T.sem[sem], 1)
+        done(q, rd, wr, (sem, CNT[sem]))
+
+    def tt(o, a, b, f):
+        op("v", [a, b], [o], lambda: g.vector.tensor_tensor(ap(o), ap(a), ap(b), f))
+
+    def ts(o, a, s1, f1, s2=None, f2=None):
+        rd = [a] + [s for s in (s1, s2) if isinstance(s, tuple)]
+        x1, x2 = [ap(s) if isinstance(s, tuple) else s for s in (s1, s2)]
+        op("v", rd, [o], lambda: g.vector.tensor_scalar(ap(o), ap(a), x1, x2, f1, *([f2] if f2 is not None else [])))
+
+    def cp(o, a):
+        op("v", [a], [o], lambda: g.vector.tensor_copy(ap(o), ap(a)))
+
+    def scan(o, d0, d1, f0=AL.add, f1=AL.max):
+        op("v", [d0, d1], [o], lambda: g.vector.tensor_tensor_scan(ap(o), ap(d0), ap(d1), 0.0, f0, f1))
+
+    def fill(o, x):
+        op("v", [], [o], lambda: g.vector.memset(ap(o), x))
+
+    def quant(qn, i):
+        a, b = R(qn), R(qn + "s")
+        op("v", [i], [a, b], lambda: g.vector.quantize_mx(ap(a), ap(b), ap(i)))
+
+    def act(o, i, f=AF.Copy, scale=None, accum=None):
+        kw = {} if scale is None else {"scale": scale}
+        if accum is not None:
+            kw["accum_out"] = ap(accum)
+        op("a", [i], [o] + ([accum] if accum else []), lambda: g.scalar.activation(ap(o), ap(i), f, **kw))
+
+    def mm(o, wn, wlo, xn, n, start=True, stop=True):
+        w, ws = R(wn, wlo, wlo + 128), R(wn + "s", wlo, wlo + 128)
+        x, xs = R(xn, 0, n), R(xn + "s", 0, n)
+        op("p", [w, ws, x, xs], [o], lambda: g.tensor.matmul_mx(ap(o), ap(w), ap(ws), ap(x), ap(xs), start, stop), loose=not start)
+
+    def iota(o, pat, cm=0, **kw):
+        op("g", [], [o], lambda: g.iota(ap(o), pat, 0, cm, **kw))
+
+    def asel(o, i, pat, f, base, cm):
+        op("g", [i], [o], lambda: g.affine_select(ap(o), ap(i), pat, f, 0.0, base, cm))
+
+    def dma(q, o, i, rd, wr, sem):
+        hold(q, rd, wr)
+        ENG[q].dma_start(o, i).then_inc(T.sem[sem], 16)
+        done(q, rd, wr, (sem, 16))
+
+    def send(to, rsem, *pairs):
+        c = T.cores[to % 8]
+        adr, ne = topo.addr(c), len(topo.engines(core, c))
+        for dst, src in pairs:
+            hold("g", [src], [])
+            CNT["ls"] += ne
+            g.remote_dma(ap(dst), ap(src), T.sem[rsem], T.sem["ls"], adr[1], adr[0], topo.mask(core, c))
+        seq[0] += 1
+        ev = (rsem, ne * len(pairs))
+        clocks[ev] = {ev[0]: ev[1], "#": seq[0]}
+        for r, src in pairs:
+            writes.setdefault(r[0], []).append((r[1:4], ev, "far"))
+
+    dma("s", ap(R("xt0")), T.x[:, :], [], [R("xt0")], "dx")
+    dma("a", ap(R("ut")), T.u[:, :], [], [R("ut")], "du")
+    dma("a", ap(R("li")), T.link[:, :], [], [R("li")], "dl")
+    dma("s", ap(R("wq", bit="u8")), T.wc[:, :], [], [R("wq")], "dw")
+    dma("s", ap(R("wqs")), T.ws[:, :], [], [R("wqs")], "ds")
+    dma("s", ap(R("vt")), T.v[:, :], [], [R("vt")], "dv")
+
+    KCB, JB, UO = R("kj", 0, 24), R("kj", 24, 36), R("pi", 4, 12)
+    fine = {"allow_small_or_imprecise_dtypes": True}
+    iota(R("pi", 0, 1), [[1, 1]], 1)
+    iota(R("ks"), [[1, 16]], **fine)
+    iota(UO, [[16, 8]])
+    iota(KCB, [[16, 24]], **fine)
+    iota(JB, [[16, 12]], **fine)
+    iota(R("ks4"), [[0, 4], [1, 4]], **fine)
+    iota(R("iota0"), [[1, 384]], **fine)
+
+    col = {n: R("cols", i, i + 1) for i, n in enumerate(("pm", "pm1", "p4", "p41", "b16", "b4", "bb", "thr", "k2", "pb4", "pbn", "z"))}
+    fill(R("one"), 1.0)
+    ts(R("pi", 1, 2), R("pi", 0, 1), 15, AL.bitwise_and)
+    ts(R("pi", 2, 3), R("pi", 0, 1), 2, AL.logical_shift_right, 3, AL.bitwise_and)
+    ts(R("pi", 3, 4), R("pi", 0, 1), 3, AL.bitwise_and)
+    fill(R("ow", 0, 24), 0.0)
+    cp(col["pm"], R("pi", 1, 2))
+    cp(col["p4"], R("pi", 2, 3))
+    ts(col["pm1"], R("pi", 1, 2), 1.0, AL.add)
+    ts(col["p41"], R("pi", 2, 3), 1.0, AL.add)
+    ts(col["b16"], col["pm"], 14.5, AL.is_lt, BV, AL.mult)
+    ts(col["b4"], col["p4"], 2.5, AL.is_lt, BV, AL.mult)
+    ts(R("pmo"), R("ow", 0, 24), col["pm"], AL.add)
+    for b in range(4):
+        act(R("iet", 512 * b, 512 * b + 512), R("one"), scale=0.0)
+    asel(R("bot"), R("one"), [[-16, 8], [0, 64]], AL.is_ge, 0, 1)
+    asel(R("bot"), R("bot"), [[16, 8], [0, 64]], AL.is_ge, 15, -1)
+    for b in range(4):
+        asel(R("iet", 512 * b + b, 512 * b + 512, 4), R("one", 0, 128), [[-1, 128]], AL.is_equal, 0, 1)
+    ts(R("ta"), R("ks"), col["pm"], AL.is_equal, 2 * BIG, AL.mult)
+    ts(R("rsw"), R("ks"), 0.5, AL.is_gt, 2 * BIG, AL.mult)
+    ts(R("r0w"), R("ks"), 0.5, AL.is_gt)
+    ts(R("mbw"), R("ta"), -BIG, AL.add)
+    ts(R("rsw"), R("rsw"), -BIG, AL.add)
+    act(R("mb"), IND(R("mbw"), R("pmo")))
+    act(R("rs"), IND(R("rsw"), R("pmo")))
+    ts(R("ta"), R("ks"), col["pm"], AL.is_equal, -2 * BV, AL.mult)
+    ts(R("tn"), R("ks"), col["pm1"], AL.is_equal, BV, AL.mult)
+    ts(R("t16w"), R("ks"), 0.5, AL.is_lt, -8 * BV, AL.mult)
+    tt(R("ta"), R("ta"), R("tn"), AL.add)
+    ts(R("uo16", 0, 8), UO, 0.0, AL.add)
+    ts(R("uo16", 8, 16), UO, 1.0, AL.add)
+    tt(R("t16w"), R("t16w"), R("ta"), AL.add)
+    ts(col["bb"], col["b16"], 2.0 ** -17, AL.mult)
+    ts(col["thr"], col["b16"], 2.0 ** -17, AL.mult, 0.5, AL.add)
+    ts(R("tbw"), R("t16w"), 2.0 ** -17, AL.mult)
+    act(R("tb"), IND(R("tbw"), R("pmo")))
+    act(R("r0"), IND(R("r0w"), R("pmo")))
+    act(R("t16"), IND(R("t16w"), R("pmo")))
+    for n, ls, w in TILES:
+        fill(R(n, 64 * ls[-1], 4 * w), 0.0)
+    fill(R("ru", 0, 1), 0.0)
+    quant("uq", R("ut"))
+    for n, lo in (("urs", 0), ("urb", 8)):
+        cp(R(n, bit="u32"), IND(R("uq", bit="u32"), R("uo16", lo, lo + 8)))
+        cp(R(n + "s"), IND(R("uqs"), R("uo16", lo, lo + 8)))
+    fill(R("zt"), 0.0)
+    fill(R("ak", 384, 512), 0.0)
+    fill(R("al", 384, 512), 0.0)
+
+    xin = "xt0"
+    for t in range(NR):
+        d = 2 ** t
+        xn, lr, qk, vb = "xt%d" % (t + 1), "lr%d" % t, "qk%d" % t, "vb%d" % t
+        sb, lb, sn, ln, st, lt = ["%s%d" % (n, t) for n in ("sb", "lb", "sn", "ln", "st", "lt")]
+        P = [R("p%d" % b, 0, 384) for b in range(8)]
+        quant("xq", R(xin))
+        mm(P[0], "urs", 0, "xq", 384)
+        mm(P[1], "urb", 0, "xq", 384)
+        if t:
+            for b in range(4):
+                mm(P[2 + b], "eq", 128 * b, "xq", 384)
+        else:
+            for k in range(NR):
+                quant("vb%d" % k, R("zt"))
+        act(R("sg"), P[1], AF.Sign)
+        tt(R("m2"), P[0], R("mb"), AL.min)
+        scan(R("hs"), R("rs"), R("m2"), AL.min)
+        scan(R("bt"), R("tb"), R("sg"))
+        ts(R(sb), R("bt", 15, 384, 16), col["thr"], AL.is_gt)
+        send(rank - d, "rb%d" % t, (R(lb), R(sb)))
+        if t:
+            for b in range(2):
+                act(R(xn, b, 1536, 4), P[2 + b])
+        tt(R("fa", 3, 1536, 4), P[0], R("hs"), AL.is_le)
+        ju = 0
+        for ti, (fn, ls, w) in enumerate(TILES):
+            for s, c in enumerate(ls):
+                n = 16 * c
+                ts(R(fn, s, 4 * n, 4), R("p0", 0, n), R("hs", n + 15, n + 16), AL.is_lt)
+                act(R("junk", ju, ju + n), R(fn, s, 4 * n, 4), accum=R("ru", c, c + 1))
+                ju += n
+            if ti == 0:
+                if t == 0:
+                    cp(R("lt16"), R("li"))
+                    cp(R("ow", 48, 72), R("li"))
+                    act(R(lr), IND(R("iota0"), R("lt16")))
+                    quant("bo", R("bot"))
+                    ts(KCB, KCB, 15.0, AL.add, col["pm"], AL.subtract)
+                    ts(JB, JB, col["pm"], AL.add, col["b16"], AL.add)
+                    ts(col["k2"], col["b16"], -1.0, AL.mult, 191.0, AL.add)
+                    ts(KCB, KCB, col["b16"], AL.subtract)
+                else:
+                    act(R("tr"), IND(R("iota0"), R("lt%d" % (t - 1))))
+                    act(R(lr), IND(R("tr"), R("lt16")))
+                scan(R("rds"), R("r0"), R("fa", 3, 1536, 4), AL.mult, AL.add)
+            quant("q" + fn, R(fn))
+            mm(R("p6", 0, w), "bo", 0, "q" + fn, w, start=ti == 0, stop=ti == 5)
+            if ti == 0:
+                tt(R("kr", 0, 24), KCB, R("rds", 15, 384, 16), AL.subtract)
+                if t == 0:
+                    ts(R("ta"), R("ks4"), col["p4"], AL.is_equal, -2 * BV, AL.mult)
+                    ts(R("tn"), R("ks4"), col["p41"], AL.is_equal, BV, AL.mult)
+                    ts(R("t4w"), R("ks4"), 0.5, AL.is_lt, -8 * BV, AL.mult)
+                    tt(R("ta"), R("ta"), R("tn"), AL.add)
+                    ts(col["pb4"], R("pi", 3, 4), -4.0, AL.add)
+                    ts(col["z"], col["b4"], -4.0, AL.mult, 4.0, AL.add)
+                    tt(R("t4w"), R("t4w"), R("ta"), AL.add)
+                    tt(col["pbn"], col["z"], col["pb4"], AL.add)
+                    ts(R("cw"), R("ks"), 2.0, AL.mult, -1.0, AL.add)
+                    ts(R("iota1"), R("iota0"), 1.0, AL.add)
+                    act(R("t4"), IND(R("t4w"), R("pmo", 0, 12)))
+            if ti == 2:
+                if t:
+                    scan(R("lc"), R("t16"), R(lr))
+                ts(R("ow", 0, 24), R("bt", 15, 384, 16), col["thr"], AL.is_gt, 384.0, AL.mult)
+                if t:
+                    ts(R("ow", 48, 72), R("lc", 15, 384, 16), col["b16"], AL.subtract)
+                    ts(R("lt16"), R("lc", 15, 384, 16), col["b16"], AL.subtract)
+            if ti == 3:
+                tt(R("ow", 24, 48), R("ow", 0, 24), R("ow", 48, 72), AL.add)
+                act(R("w2", 0, 384), IND(R("cw"), R(lb)), scale=-1.0)
+                act(R("w2", 384, 768), IND(R("cw"), R(lb)))
+            if ti == 4:
+                cp(R("off16"), R("ow", 24, 48))
+        if t == 0:
+            quant("eq", R("iet"))
+            for b in range(4):
+                mm(P[2 + b], "eq", 128 * b, "xq", 384)
+        tt(R("pay"), IND(R("w2"), R("off16")), R("iota1"), AL.mult)
+        scan(R("mc"), R("t16"), P[6])
+        tt(R("kr", 24, 48), R("kr", 0, 24), R("ru"), AL.subtract)
+        tt(R("kr", 48, 72), R("mc", 15, 384, 16), R("kr", 24, 48), AL.add)
+        cp(R("rk16"), R("kr", 48, 72))
+        cp(IND(R("sp"), R("rk16")), R("pay"))
+        for b in range(2 if t else 0, 4):
+            act(R(xn, b, 1536, 4), P[2 + b])
+        ts(R("fl"), R("sp", 1, 384, 2), 0.0, AL.is_lt)
+        act(R("kaqa", 0, 192), R("sp", 0, 384, 2), AF.Abs)
+        act(R("kaqa", 192, 384), R("sp", 1, 384, 2), AF.Abs, scale=512.0)
+        act(R("fh"), R(xn), scale=0.5)
+        scan(R("fcum"), R("fl"), R("fl"))
+        scan(R("flc"), R("tb", 0, 192), R("fl"))
+        scan(R("fc2"), R("t16", 0, 192), R("fcum"))
+        flt, pp1, pp2, pp3, nn = [R("pp", 12 * i, 12 * i + 12) for i in range(5)]
+        ts(flt, R("flc", 15, 192, 16), col["bb"], AL.subtract)
+        ts(pp2, R("fc2", 15, 192, 16), R("fcum", 191, 192), AL.subtract, col["k2"], AL.add)
+        tt(pp1, JB, R("fc2", 15, 192, 16), AL.subtract)
+        tt(pp3, pp2, flt, AL.mult)
+        tt(R("kq"), R("kaqa", 0, 192), R("kaqa", 192, 384), AL.add)
+        tt(nn, pp1, pp3, AL.max)
+        cp(R("n16"), nn)
+        cp(IND(R("kqs"), R("n16")), R("kq"))
+        scan(R("c16"), R("t16", 0, 192), R("kqs"))
+        scan(R("c4"), R("t4"), R("kqs"))
+        ts(R("kqi", 48, 60), R("c16", 15, 192, 16), col["b16"], AL.subtract)
+        ts(R("kqi", 0, 48), R("c4", 3, 192, 4), col["b4"], AL.subtract)
+        ts(R("kqi", 60, 120), R("kqi", 0, 60), 9, AL.logical_shift_right)
+        ts(R("kqi", 120, 180), R("kqi", 0, 60), 511, AL.bitwise_and)
+        ts(R("t4q"), R("kqi", 60, 108), 4.0, AL.mult, col["pb4"], AL.add)
+        ts(R("tqk"), R("kqi", 108, 114), -1.0, AL.add)
+        ts(R("t4k"), R("kqi", 120, 168), 4.0, AL.mult, col["pb4"], AL.add)
+        act(R("fq", 0, 192), IND(R("fh"), R("t4q", 0, 12)))
+        act(R("fq", 192, 384), IND(R("fh"), R("t4q", 12, 24)))
+        act(R("fq", 384, 768), IND(R("fh"), R("t4q", 24, 48)))
+        cp(R("lqk"), IND(R(lr), R("tqk")))
+        ts(R("tll", 0, 6), R("kqi", 114, 120), -1.0, AL.add)
+        tt(R("ak", 0, 192), IND(R("fh"), R("t4k", 0, 12)), R("fq", 0, 192), AL.add)
+        scan(R("nmc"), R("t4", 0, 96), R("lqk"))
+        ts(R("tll", 6, 12), R("kqi", 174, 180), -1.0, AL.add)
+        ts(R(sn), R("nmc", 3, 96, 4), 4.0, AL.mult, col["pbn"], AL.add)
+        send(rank + d, "rn%d" % t, (R(ln), R(sn)))
+        tt(R("ak", 192, 384), IND(R("fh"), R("t4k", 12, 24)), R("fq", 192, 384), AL.add)
+        quant(qk, R("ak"))
+        send(rank + d, "rc%d" % t, (R(vb, 0, 96, 1, "u8"), R(qk, 0, 96, 1, "u8")), (R(vb + "s", 0, 96), R(qk + "s", 0, 96)))
+        tt(R("al", 0, 384), IND(R("fh"), R("t4k", 24, 48)), R("fq", 384, 768), AL.add)
+        quant("ql", R("al"))
+        act(R("val", 0, 96), IND(R(lr), R("tll", 6, 12)))
+        act(R("val", 96, 192), IND(R(lr), R("tll", 0, 6)))
+        act(R("tu"), R(lr))
+        act(R("fl32"), R("fq", 384, 768), scale=64.0)
+        left = ("p0", "p1", "p6", "p7")
+        for b in range(4):
+            mm(R(left[b], 0, 128), "wq", 128 * b, "ql", 128)
+        cp(IND(R("tu"), R("tll")), R("val"))
+        for b in range(4):
+            tt(R("sl", b, 384, 4), R(left[b], 0, 96), R("fl32", b, 384, 4), AL.add)
+        act(R("rl"), R("sl"), scale=0.03125)
+        scan(R("tuc"), R("t16"), R("tu"))
+        if t == 0:
+            quant("vq", R("vt"))
+        ts(R(st), R("tuc", 15, 384, 16), col["b16"], AL.subtract)
+        send(rank - d, "rt%d" % t, (R(lt), R(st)))
+        cp(IND(R(xn), R("t4q", 24, 48)), R("rl"))
+        act(R("fn32"), IND(R("fh"), R(ln)), scale=64.0)
+        for b in range(4):
+            mm(R("p%d" % (2 + b), 0, 128), "wq", 128 * b, vb, 128)
+        for b in range(4):
+            tt(R("sa", b, 384, 4), R("p%d" % (2 + b), 0, 96), R("fn32", b, 384, 4), AL.add)
+            act(R("ra", b, 384, 4), R("sa", b, 384, 4), scale=0.03125)
+        cp(IND(R(xn), R(ln)), R("ra"))
+        xin = xn
+    quant("xq", R(xin))
+    act(R("tr"), IND(R("iota0"), R("lt2")))
+    act(R("lr3"), IND(R("tr"), R("lt16")))
+    mm(R("p0", 0, 384), "vq", 0, "xq", 384)
+    dma("s", T.lk[:, :], T.lr3[0:128:16, :], [R("lr3")], [], "ok")
+    dma("s", T.oc[:, :], ap(R("xq", bit="u8")), [R("xq")], [], "oc_")
+    for k in range(4):
+        dma("s", T.osc[4 * k:4 * k + 4, :], T.xqs[32 * k:32 * k + 4, 0:384], [R("xqs")], [], "o%d" % k)
+    act(R("ys"), R("p0", 0, 384))
+    dma("a", T.y[:, :], ap(R("ys")), [R("ys")], [], "oy")
+    for s in ("oc_", "o0", "o1", "o2", "o3", "oy", "ok"):
+        g.wait_ge(T.sem[s], 16)
+    for s in ("v", "a", "p", "gc", "ls"):
+        g.wait_ge(T.sem[s], CNT[s])

@@ -3,7 +3,7 @@ from concourse.mybir import dt, AluOpType, ActivationFunctionType
 AL, AF = AluOpType, ActivationFunctionType
 NR = 3
 BIG = 1.0e29
-BV = float(2 ** 19)
+BV = float(2 ** 20)
 TILES = [("fa", [23, 22, 21], 384), ("fb", [20, 19, 18, 17], 320), ("fc", [16, 15, 14, 13], 256),
          ("fd", [12, 11, 10, 9], 192), ("fe", [8, 7, 6, 5], 128), ("ff", [4, 3, 2, 1], 128)]
 
@@ -29,8 +29,8 @@ def _each(text, dtype):
 
 
 _each("xt0:1536 xt1:1536 xt2:1536 xt3:1536 fh:1536 ut:512 vt:512 iet:2048 bot:512 zt:512 ak:512 al:512 one:512 sg:384 bt:384 rds:384 "
-      "r0:384 tb:384 w2:768 fl:192 flc:192 junk:4416 rl:384 ra:384", "bfloat16")
-_s([("r0w", 16), ("tbw", 16), ("cw", 16)], "bfloat16", buf="kb")
+      "r0:384 tb:384 w2:768 fl:192 flc:192 junk:4416 rl:384 ra:384 sgl:1104", "bfloat16")
+_s([("r0w", 16), ("tbw", 16), ("cw", 16), ("cv", 16)], "bfloat16", buf="kb")
 _s([(_n, 4 * _w) for _n, _l, _w in TILES], "bfloat16", buf="ft")
 _s([("q" + _n, _w) for _n, _l, _w in TILES], "codes", buf="qf")
 _each("xq:384 uq:128 urs:128 urb:128 vq:128 eq:512 bo:128 wq:512 ql:128", "codes")
@@ -39,15 +39,15 @@ for _t in "012":
     _each(" ".join(_n + _t + ":24" for _n in ("sb", "lb", "sn", "ln", "st", "lt")), "uint16")
 _s([(_n, 16) for _n in ("ks", "ks4", "mbw", "rsw", "t16w", "t4w", "ta", "tn", "cols")], "float32", buf="kw")
 _s([("c4", 192), ("c16", 192), ("fc2", 192), ("fcum", 192)], "float32", buf="cc")
-_s([("kq", 192), ("lqk", 96), ("nmc", 96)], "float32", buf="kn")
+_s([("kq", 384), ("lqk", 96), ("nmc", 96)], "float32", buf="kn")
 _s([("mc", 384), ("tuc", 384), ("lc", 384)], "float32", buf="sc3")
-_each("kj:36 iota0:384 iota1:384 mb:384 rs:384 t16:384 t4:192 m2:384 hs:384 ru:24 kr:72 ow:72 pay:384 sp:384 kaqa:384 kqs:192 pp:60 "
+_each("kj:36 iota0:384 alt:384 mb:384 rs:384 t16:384 t4:192 m2:384 hs:384 ru:24 kr:72 ow:72 pay:384 sp:384 kqs:192 pp:60 "
       "fq:768 fl32:384 fn32:384 sl:384 sa:384 val:192 tu:384 tr:384 lr0:384 lr1:384 lr2:384 lr3:384 ys:384", "float32")
 _each("li:24 pi:12 kqi:180", "int32")
 _each("pmo:24 uo16:16 lt16:24 off16:24 rk16:24 n16:12 t4q:48 t4k:48 tqk:6 tll:12", "uint16")
 _s([("p%d" % _b, 512) for _b in range(8)], "float32", "psum", "ps")
 
-SEMAPHORES = "v a p gc ls dx du dw ds dv dl oy ok oc_ o0 o1 o2 o3 rb0 rb1 rb2 rn0 rn1 rn2 rc0 rc1 rc2 rt0 rt1 rt2".split()
+SEMAPHORES = "v a p gc ls dx du dw ds dv dl oy oz ok oc_ o0 o1 o2 o3 rb0 rb1 rb2 rn0 rn1 rn2 rc0 rc1 rc2 rt0 rt1 rt2".split()
 
 
 def R(name, lo=0, hi=None, step=1, bit=None):
@@ -144,15 +144,17 @@ def rank_program(g, core, T, topo):
         a, b = R(qn), R(qn + "s")
         op("v", [i], [a, b], lambda: g.vector.quantize_mx(ap(a), ap(b), ap(i)))
 
-    def act(o, i, f=AF.Copy, scale=None, accum=None):
+    def act(o, i, f=AF.Copy, scale=None, accum=None, bias=None):
         kw = {} if scale is None else {"scale": scale}
+        if bias is not None:
+            kw["bias"] = ap(bias)
         if accum is not None:
             kw["accum_out"] = ap(accum)
-        op("a", [i], [o] + ([accum] if accum else []), lambda: g.scalar.activation(ap(o), ap(i), f, **kw))
+        op("a", [i] + ([bias] if bias else []), [o] + ([accum] if accum else []), lambda: g.scalar.activation(ap(o), ap(i), f, **kw))
 
-    def mm(o, wn, wlo, xn, n, start=True, stop=True):
+    def mm(o, wn, wlo, xn, n, start=True, stop=True, lo=0):
         w, ws = R(wn, wlo, wlo + 128), R(wn + "s", wlo, wlo + 128)
-        x, xs = R(xn, 0, n), R(xn + "s", 0, n)
+        x, xs = R(xn, lo, lo + n), R(xn + "s", lo, lo + n)
         op("p", [w, ws, x, xs], [o], lambda: g.tensor.matmul_mx(ap(o), ap(w), ap(ws), ap(x), ap(xs), start, stop), loose=not start)
 
     def iota(o, pat, cm=0, **kw):
@@ -195,6 +197,7 @@ def rank_program(g, core, T, topo):
     iota(JB, [[16, 12]], **fine)
     iota(R("ks4"), [[0, 4], [1, 4]], **fine)
     iota(R("iota0"), [[1, 384]], **fine)
+    iota(R("alt"), [[0, 192], [1024, 2]], **fine)
 
     col = {n: R("cols", i, i + 1) for i, n in enumerate(("pm", "pm1", "p4", "p41", "b16", "b4", "bb", "thr", "k2", "pb4", "pbn", "z"))}
     fill(R("one"), 1.0)
@@ -229,13 +232,13 @@ def rank_program(g, core, T, topo):
     ts(R("uo16", 0, 8), UO, 0.0, AL.add)
     ts(R("uo16", 8, 16), UO, 1.0, AL.add)
     tt(R("t16w"), R("t16w"), R("ta"), AL.add)
-    ts(col["bb"], col["b16"], 2.0 ** -17, AL.mult)
-    ts(col["thr"], col["b16"], 2.0 ** -17, AL.mult, 0.5, AL.add)
-    ts(R("tbw"), R("t16w"), 2.0 ** -17, AL.mult)
+    ts(col["bb"], col["b16"], 2.0 ** -18, AL.mult)
+    ts(col["thr"], col["b16"], 2.0 ** -18, AL.mult, 0.5, AL.add)
+    ts(R("tbw"), R("t16w"), 2.0 ** -18, AL.mult)
     act(R("tb"), IND(R("tbw"), R("pmo")))
     act(R("r0"), IND(R("r0w"), R("pmo")))
     act(R("t16"), IND(R("t16w"), R("pmo")))
-    for n, ls, w in TILES:
+    for n, ls, w in TILES[:2]:
         fill(R(n, 64 * ls[-1], 4 * w), 0.0)
     fill(R("ru", 0, 1), 0.0)
     quant("uq", R("ut"))
@@ -255,43 +258,64 @@ def rank_program(g, core, T, topo):
         quant("xq", R(xin))
         mm(P[0], "urs", 0, "xq", 384)
         mm(P[1], "urb", 0, "xq", 384)
+        mm(P[7], "urs", 0, "xq", 384)
         if t:
             for b in range(4):
                 mm(P[2 + b], "eq", 128 * b, "xq", 384)
+            scan(R("lc"), R("t16"), R(lr))
         else:
             for k in range(NR):
                 quant("vb%d" % k, R("zt"))
         act(R("sg"), P[1], AF.Sign)
         tt(R("m2"), P[0], R("mb"), AL.min)
+        if t:
+            ts(R("ow", 48, 72), R("lc", 15, 384, 16), col["b16"], AL.subtract)
+            ts(R("lt16"), R("lc", 15, 384, 16), col["b16"], AL.subtract)
+        else:
+            cp(R("lt16"), R("li"))
+            cp(R("ow", 48, 72), R("li"))
         scan(R("hs"), R("rs"), R("m2"), AL.min)
         scan(R("bt"), R("tb"), R("sg"))
+        tt(R("fa", 3, 1536, 4), P[0], R("hs"), AL.is_le)
         ts(R(sb), R("bt", 15, 384, 16), col["thr"], AL.is_gt)
         send(rank - d, "rb%d" % t, (R(lb), R(sb)))
+        for n, ls, w in TILES[2:] if t == 0 else []:
+            iota(R(n, 64 * ls[-1], 4 * w), [[0, 4 * w - 64 * ls[-1]]], **fine)
         if t:
             for b in range(2):
                 act(R(xn, b, 1536, 4), P[2 + b])
-        tt(R("fa", 3, 1536, 4), P[0], R("hs"), AL.is_le)
-        ju = 0
+        for k, c in enumerate((23, 22, 21)):
+            act(R("sgl", 368 * k, 368 * k + 16 * c), R("p7", 0, 16 * c), AF.Sign, scale=-1.0, bias=R("hs", 16 * c + 15, 16 * c + 16))
+        ju = [0]
+
+        def layer(fn, k, c, by=None):
+            n = 16 * c
+            if by is None:
+                ts(R(fn, k, 4 * n, 4), R("p0", 0, n), R("hs", n + 15, n + 16), AL.is_lt)
+            else:
+                ts(R(fn, k, 4 * n, 4), R("sgl", 368 * by, 368 * by + n), 0.5, AL.is_gt)
+            act(R("junk", ju[0], ju[0] + n), R(fn, k, 4 * n, 4), accum=R("ru", c, c + 1))
+            ju[0] += n
+
+        for k in range(4):
+            layer("fb", k, 20 - k)
+        for k in range(3):
+            layer("fa", k, 23 - k, k)
         for ti, (fn, ls, w) in enumerate(TILES):
-            for s, c in enumerate(ls):
-                n = 16 * c
-                ts(R(fn, s, 4 * n, 4), R("p0", 0, n), R("hs", n + 15, n + 16), AL.is_lt)
-                act(R("junk", ju, ju + n), R(fn, s, 4 * n, 4), accum=R("ru", c, c + 1))
-                ju += n
+            todo = [(TILES[ti + 1][0], k, c) for k, c in enumerate(TILES[ti + 1][1]) if c < 17] if ti < 5 else []
+            for x in todo[:1]:
+                layer(*x)
             if ti == 0:
                 if t == 0:
-                    cp(R("lt16"), R("li"))
-                    cp(R("ow", 48, 72), R("li"))
                     act(R(lr), IND(R("iota0"), R("lt16")))
                     quant("bo", R("bot"))
                     ts(KCB, KCB, 15.0, AL.add, col["pm"], AL.subtract)
                     ts(JB, JB, col["pm"], AL.add, col["b16"], AL.add)
                     ts(col["k2"], col["b16"], -1.0, AL.mult, 191.0, AL.add)
                     ts(KCB, KCB, col["b16"], AL.subtract)
-                else:
-                    act(R("tr"), IND(R("iota0"), R("lt%d" % (t - 1))))
-                    act(R(lr), IND(R("tr"), R("lt16")))
                 scan(R("rds"), R("r0"), R("fa", 3, 1536, 4), AL.mult, AL.add)
+            if ti == 5:
+                cp(R("off16"), R("ow", 24, 48))
             quant("q" + fn, R(fn))
             mm(R("p6", 0, w), "bo", 0, "q" + fn, w, start=ti == 0, stop=ti == 5)
             if ti == 0:
@@ -301,31 +325,26 @@ def rank_program(g, core, T, topo):
                     ts(R("tn"), R("ks4"), col["p41"], AL.is_equal, BV, AL.mult)
                     ts(R("t4w"), R("ks4"), 0.5, AL.is_lt, -8 * BV, AL.mult)
                     tt(R("ta"), R("ta"), R("tn"), AL.add)
-                    ts(col["pb4"], R("pi", 3, 4), -4.0, AL.add)
-                    ts(col["z"], col["b4"], -4.0, AL.mult, 4.0, AL.add)
+                    cp(col["pb4"], R("pi", 3, 4))
+                    ts(col["z"], col["b4"], -4.0, AL.mult)
                     tt(R("t4w"), R("t4w"), R("ta"), AL.add)
                     tt(col["pbn"], col["z"], col["pb4"], AL.add)
-                    ts(R("cw"), R("ks"), 2.0, AL.mult, -1.0, AL.add)
-                    ts(R("iota1"), R("iota0"), 1.0, AL.add)
+                    ts(R("cw"), R("ks"), 512.0, AL.mult)
+                    ts(R("cv"), R("ks"), -512.0, AL.mult, 512.0, AL.add)
                     act(R("t4"), IND(R("t4w"), R("pmo", 0, 12)))
             if ti == 2:
-                if t:
-                    scan(R("lc"), R("t16"), R(lr))
+                act(R("w2", 0, 384), IND(R("cw"), R(lb)))
+                act(R("w2", 384, 768), IND(R("cv"), R(lb)))
                 ts(R("ow", 0, 24), R("bt", 15, 384, 16), col["thr"], AL.is_gt, 384.0, AL.mult)
-                if t:
-                    ts(R("ow", 48, 72), R("lc", 15, 384, 16), col["b16"], AL.subtract)
-                    ts(R("lt16"), R("lc", 15, 384, 16), col["b16"], AL.subtract)
             if ti == 3:
                 tt(R("ow", 24, 48), R("ow", 0, 24), R("ow", 48, 72), AL.add)
-                act(R("w2", 0, 384), IND(R("cw"), R(lb)), scale=-1.0)
-                act(R("w2", 384, 768), IND(R("cw"), R(lb)))
-            if ti == 4:
-                cp(R("off16"), R("ow", 24, 48))
+            for x in todo[1:]:
+                layer(*x)
         if t == 0:
             quant("eq", R("iet"))
             for b in range(4):
                 mm(P[2 + b], "eq", 128 * b, "xq", 384)
-        tt(R("pay"), IND(R("w2"), R("off16")), R("iota1"), AL.mult)
+        tt(R("pay"), IND(R("w2"), R("off16")), R("iota0"), AL.add)
         scan(R("mc"), R("t16"), P[6])
         tt(R("kr", 24, 48), R("kr", 0, 24), R("ru"), AL.subtract)
         tt(R("kr", 48, 72), R("mc", 15, 384, 16), R("kr", 24, 48), AL.add)
@@ -333,42 +352,48 @@ def rank_program(g, core, T, topo):
         cp(IND(R("sp"), R("rk16")), R("pay"))
         for b in range(2 if t else 0, 4):
             act(R(xn, b, 1536, 4), P[2 + b])
-        ts(R("fl"), R("sp", 1, 384, 2), 0.0, AL.is_lt)
-        act(R("kaqa", 0, 192), R("sp", 0, 384, 2), AF.Abs)
-        act(R("kaqa", 192, 384), R("sp", 1, 384, 2), AF.Abs, scale=512.0)
         act(R("fh"), R(xn), scale=0.5)
+
+        def pairs(a, b):
+            scan(R("kq", a, b), R("alt", a, b), R("sp", a, b), AL.mult, AL.add)
+
+        flt, pp1, pp2, pp3, nn = [R("pp", 12 * i, 12 * i + 12) for i in range(5)]
+        ts(R("fl"), R("sp", 1, 384, 2), 511.5, AL.is_gt)
+        pairs(0, 128)
         scan(R("fcum"), R("fl"), R("fl"))
         scan(R("flc"), R("tb", 0, 192), R("fl"))
         scan(R("fc2"), R("t16", 0, 192), R("fcum"))
-        flt, pp1, pp2, pp3, nn = [R("pp", 12 * i, 12 * i + 12) for i in range(5)]
         ts(flt, R("flc", 15, 192, 16), col["bb"], AL.subtract)
         ts(pp2, R("fc2", 15, 192, 16), R("fcum", 191, 192), AL.subtract, col["k2"], AL.add)
         tt(pp1, JB, R("fc2", 15, 192, 16), AL.subtract)
         tt(pp3, pp2, flt, AL.mult)
-        tt(R("kq"), R("kaqa", 0, 192), R("kaqa", 192, 384), AL.add)
+        pairs(128, 256)
         tt(nn, pp1, pp3, AL.max)
+        pairs(256, 384)
         cp(R("n16"), nn)
-        cp(IND(R("kqs"), R("n16")), R("kq"))
-        scan(R("c16"), R("t16", 0, 192), R("kqs"))
+        cp(IND(R("kqs"), R("n16")), R("kq", 1, 384, 2))
         scan(R("c4"), R("t4"), R("kqs"))
-        ts(R("kqi", 48, 60), R("c16", 15, 192, 16), col["b16"], AL.subtract)
+        scan(R("c16"), R("t16", 0, 192), R("kqs"))
         ts(R("kqi", 0, 48), R("c4", 3, 192, 4), col["b4"], AL.subtract)
-        ts(R("kqi", 60, 120), R("kqi", 0, 60), 9, AL.logical_shift_right)
-        ts(R("kqi", 120, 180), R("kqi", 0, 60), 511, AL.bitwise_and)
+        ts(R("kqi", 48, 60), R("c16", 15, 192, 16), col["b16"], AL.subtract)
+        ts(R("kqi", 60, 108), R("kqi", 0, 48), 511, AL.bitwise_and)
+        ts(R("kqi", 120, 168), R("kqi", 0, 48), 10, AL.logical_shift_right, 511, AL.bitwise_and)
         ts(R("t4q"), R("kqi", 60, 108), 4.0, AL.mult, col["pb4"], AL.add)
-        ts(R("tqk"), R("kqi", 108, 114), -1.0, AL.add)
+        ts(R("kqi", 108, 120), R("kqi", 48, 60), 511, AL.bitwise_and)
         ts(R("t4k"), R("kqi", 120, 168), 4.0, AL.mult, col["pb4"], AL.add)
+        cp(R("tqk"), R("kqi", 108, 114))
+        ts(R("kqi", 168, 180), R("kqi", 48, 60), 10, AL.logical_shift_right, 511, AL.bitwise_and)
         act(R("fq", 0, 192), IND(R("fh"), R("t4q", 0, 12)))
         act(R("fq", 192, 384), IND(R("fh"), R("t4q", 12, 24)))
         act(R("fq", 384, 768), IND(R("fh"), R("t4q", 24, 48)))
         cp(R("lqk"), IND(R(lr), R("tqk")))
-        ts(R("tll", 0, 6), R("kqi", 114, 120), -1.0, AL.add)
         tt(R("ak", 0, 192), IND(R("fh"), R("t4k", 0, 12)), R("fq", 0, 192), AL.add)
         scan(R("nmc"), R("t4", 0, 96), R("lqk"))
-        ts(R("tll", 6, 12), R("kqi", 174, 180), -1.0, AL.add)
+        cp(R("tll", 0, 6), R("kqi", 114, 120))
         ts(R(sn), R("nmc", 3, 96, 4), 4.0, AL.mult, col["pbn"], AL.add)
         send(rank + d, "rn%d" % t, (R(ln), R(sn)))
         tt(R("ak", 192, 384), IND(R("fh"), R("t4k", 12, 24)), R("fq", 192, 384), AL.add)
+        cp(R("tll", 6, 12), R("kqi", 174, 180))
         quant(qk, R("ak"))
         send(rank + d, "rc%d" % t, (R(vb, 0, 96, 1, "u8"), R(qk, 0, 96, 1, "u8")), (R(vb + "s", 0, 96), R(qk + "s", 0, 96)))
         tt(R("al", 0, 384), IND(R("fh"), R("t4k", 24, 48)), R("fq", 384, 768), AL.add)
@@ -396,19 +421,22 @@ def rank_program(g, core, T, topo):
         for b in range(4):
             tt(R("sa", b, 384, 4), R("p%d" % (2 + b), 0, 96), R("fn32", b, 384, 4), AL.add)
             act(R("ra", b, 384, 4), R("sa", b, 384, 4), scale=0.03125)
+        act(R("tr"), IND(R("iota0"), R(lt)))
+        act(R("lr%d" % (t + 1)), IND(R("tr"), R("lt16")))
         cp(IND(R(xn), R(ln)), R("ra"))
         xin = xn
     quant("xq", R(xin))
-    act(R("tr"), IND(R("iota0"), R("lt2")))
-    act(R("lr3"), IND(R("tr"), R("lt16")))
-    mm(R("p0", 0, 384), "vq", 0, "xq", 384)
-    dma("s", T.lk[:, :], T.lr3[0:128:16, :], [R("lr3")], [], "ok")
+    for b in range(2):
+        mm(R("p%d" % b, 0, 192), "vq", 0, "xq", 192, lo=192 * b)
     dma("s", T.oc[:, :], ap(R("xq", bit="u8")), [R("xq")], [], "oc_")
     for k in range(4):
         dma("s", T.osc[4 * k:4 * k + 4, :], T.xqs[32 * k:32 * k + 4, 0:384], [R("xqs")], [], "o%d" % k)
-    act(R("ys"), R("p0", 0, 384))
-    dma("a", T.y[:, :], ap(R("ys")), [R("ys")], [], "oy")
-    for s in ("oc_", "o0", "o1", "o2", "o3", "oy", "ok"):
+    dma("s", T.lk[:, :], T.lr3[0:128:16, :], [R("lr3")], [], "ok")
+    act(R("ys", 0, 192), R("p0", 0, 192))
+    dma("a", T.y[:, 0:192], ap(R("ys", 0, 192)), [R("ys", 0, 192)], [], "oy")
+    cp(R("ys", 192, 384), R("p1", 0, 192))
+    dma("s", T.y[:, 192:384], ap(R("ys", 192, 384)), [R("ys", 192, 384)], [], "oz")
+    for s in ("oc_", "o0", "o1", "o2", "o3", "oy", "oz", "ok"):
         g.wait_ge(T.sem[s], 16)
     for s in ("v", "a", "p", "gc", "ls"):
         g.wait_ge(T.sem[s], CNT[s])

from concourse.mybir import dt, AluOpType, ActivationFunctionType

AL, AF = AluOpType, ActivationFunctionType
NR = 3
BIG = 1.0e29
BV = float(2 ** 20)
TILES = [("fa", [23, 22, 21], 384), ("fb", [20, 19, 18, 17], 320), ("fc", [16, 15, 14, 13], 256),
         ("fd", [12, 11, 10, 9], 192), ("fe", [8, 7, 6, 5], 128), ("ff", [4, 3, 2, 1], 128)]

SCRATCH, WHERE = {}, {}


def _s(names, dtype, where="sbuf", buf=None):
    buf, n = buf or names[0][0], 0
    for name, w in names:
        WHERE[name] = (buf, n, w)
        if dtype == "codes":
            WHERE[name + "s"] = (buf + "s", n, w)
        n += w
    SCRATCH[buf] = (where, [128, n], "float8_e4m3fn_x4" if dtype == "codes" else dtype)
    if dtype == "codes":
        SCRATCH[buf + "s"] = (where, [128, n], "uint8")


def _each(text, dtype):
    for w in text.split():
        n, c = w.split(":")
        _s([(n, int(c))], dtype)


_each("xt0:1536 xt1:1536 xt2:1536 xt3:1536 fh:1536 ut:512 vt:512 iet:2048 bot:512 zt:512 ak:512 al:512 one:512 sg:384 bt:384 rds:384 "
      "r0:384 tb:384 w2:768 fl:192 flc:192 junk:4416 rl:384 ra:384 sgl:1104", "bfloat16")
_s([("r0w", 16), ("tbw", 16), ("cw", 16), ("cv", 16)], "bfloat16", buf="kb")
_s([(_n, 4 * _w) for _n, _l, _w in TILES], "bfloat16", buf="ft")
_s([("q" + _n, _w) for _n, _l, _w in TILES], "codes", buf="qf")
_each("xq:384 uq:128 urs:128 urb:128 vq:128 eq:512 bo:128 wq:512 ql:128", "codes")
for _t in "012":
    _each("qk%s:128 vb%s:128" % (_t, _t), "codes")
    _each(" ".join(_n + _t + ":24" for _n in ("sb", "lb", "sn", "ln", "st", "lt")), "uint16")
_s([(_n, 16) for _n in ("ks", "ks4", "mbw", "rsw", "t16w", "t4w", "ta", "tn", "cols")], "float32", buf="kw")
_s([("c4", 192), ("c16", 192), ("fc2", 192), ("fcum", 192)], "float32", buf="cc")
_s([("kq", 384), ("lqk", 96), ("nmc", 96)], "float32", buf="kn")
_s([("mc", 384), ("tuc", 384), ("lc", 384)], "float32", buf="sc3")
_each("kj:36 iota0:384 alt:384 mb:384 rs:384 t16:384 t4:192 m2:384 hs:384 ru:24 kr:72 ow:72 pay:384 sp:384 kqs:192 pp:60 "
      "fq:768 fl32:384 fn32:384 sl:384 sa:384 val:192 tu:384 tr:384 lr0:384 lr1:384 lr2:384 lr3:384 ys:384", "float32")
_each("li:24 pi:12 kqi:180", "int32")
_each("pmo:24 uo16:16 lt16:24 off16:24 rk16:24 n16:12 t4q:48 t4k:48 tqk:6 tll:12", "uint16")
_s([("p%d" % _b, 512) for _b in range(8)], "float32", "psum", "ps")

SEMAPHORES = "v a p gc ls dx du dw ds dv dl oy oz ok oc_ o0 o1 o2 o3 rb0 rb1 rb2 rn0 rn1 rn2 rc0 rc1 rc2 rt0 rt1 rt2".split()


def R(name, lo=0, hi=None, step=1, bit=None):
    buf, at, w = WHERE[name]
    return (buf, at + lo, at + (w if hi is None else hi), step, bit)


def IND(win, off):
    return ("ind", win, off)


def flat(rs):
    return [x for r in rs for x in (r[1:] if r[0] == "ind" else (r,))]


def meets(x, y):
    if x[1] <= y[0] or y[1] <= x[0]:
        return False
    return not (x[2] == y[2] and x[2] > 1 and (x[0] - y[0]) % x[2])


def rank_program(g, core, T, topo):
    rank = T.rank_of(core)
    if rank is None:
        return
    ENG = {"v": g.vector, "a": g.scalar, "p": g.tensor, "g": g, "s": g.sync}
    CNT = {"v": 0, "a": 0, "p": 0, "gc": 0, "ls": 0}
    know = {q: {} for q in ENG}
    clocks, writes, reads, seq = {}, {}, {}, [0]

    def ap(r):
        if r[0] == "ind":
            return ap(r[1]).indirect(ap(r[2]))
        n, lo, hi, st, bit = r
        w = T[n][:, lo:hi] if st == 1 else T[n][:, lo:hi:st]
        return w if bit is None else w.bitcast(dt.uint8 if bit == "u8" else dt.uint32)

    def hold(q, rd, wr, loose=False):
        need = {}
        for r in flat(rd):
            for x, ev, own in writes.get(r[0], []):
                if meets(x, r[1:4]):
                    need[ev] = 1
        for r in flat(wr):
            for x, ev, own in writes.get(r[0], []) + reads.get(r[0], []):
                if meets(x, r[1:4]) and not (loose and own == q):
                    need[ev] = 1
        for ev in sorted(need, key=lambda e: -clocks[e]["#"]):
            if know[q].get(ev[0], 0) < ev[1]:
                ENG[q].wait_ge(T.sem[ev[0]], ev[1])
                for k, n in clocks[ev].items():
                    if know[q].get(k, 0) < n:
                        know[q][k] = n

    def done(q, rd, wr, ev):
        c = dict(know[q])
        seq[0] += 1
        c.update({ev[0]: max(c.get(ev[0], 0), ev[1]), "#": seq[0]})
        clocks[ev] = c
        for r in flat(rd):
            reads.setdefault(r[0], []).append((r[1:4], ev, q))
        for r in flat(wr):
            x = r[1:4]
            if x[2] == 1:
                for d in (writes, reads):
                    d[r[0]] = [e for e in d.get(r[0], []) if not (x[0] <= e[0][0] and e[0][1] <= x[1])]
            writes.setdefault(r[0], []).append((x, ev, q))

    def op(q, rd, wr, call, loose=False):
        hold(q, rd, wr, loose)
        sem = "gc" if q == "g" else q
        CNT[sem] += 1
        call().then_inc(T.sem[sem], 1)
        done(q, rd, wr, (sem, CNT[sem]))

    def tt(o, a, b, f):
        op("v", [a, b], [o], lambda: g.vector.tensor_tensor(ap(o), ap(a), ap(b), f))

    def ts(o, a, s1, f1, s2=None, f2=None):
        rd = [a] + [s for s in (s1, s2) if isinstance(s, tuple)]
        x1, x2 = [ap(s) if isinstance(s, tuple) else s for s in (s1, s2)]
        op("v", rd, [o], lambda: g.vector.tensor_scalar(ap(o), ap(a), x1, x2, f1, *([f2] if f2 is not None else [])))

    def cp(o, a):
        op("v", [a], [o], lambda: g.vector.tensor_copy(ap(o), ap(a)))

    def scan(o, d0, d1, f0=AL.add, f1=AL.max):
        op("v", [d0, d1], [o], lambda: g.vector.tensor_tensor_scan(ap(o), ap(d0), ap(d1), 0.0, f0, f1))

    def fill(o, x):
        op("v", [], [o], lambda: g.vector.memset(ap(o), x))

    def quant(qn, i):
        a, b = R(qn), R(qn + "s")
        op("v", [i], [a, b], lambda: g.vector.quantize_mx(ap(a), ap(b), ap(i)))

    def act(o, i, f=AF.Copy, scale=None, accum=None, bias=None):
        kw = {} if scale is None else {"scale": scale}
        if bias is not None:
            kw["bias"] = ap(bias)
        if accum is not None:
            kw["accum_out"] = ap(accum)
        op("a", [i] + ([bias] if bias else []), [o] + ([accum] if accum else []), lambda: g.scalar.activation(ap(o), ap(i), f, **kw))

    def mm(o, wn, wlo, xn, n, start=True, stop=True, lo=0):
        w, ws = R(wn, wlo, wlo + 128), R(wn + "s", wlo, wlo + 128)
        x, xs = R(xn, lo, lo + n), R(xn + "s", lo, lo + n)
        op("p", [w, ws, x, xs], [o], lambda: g.tensor.matmul_mx(ap(o), ap(w), ap(ws), ap(x), ap(xs), start, stop), loose=not start)

    def iota(o, pat, cm=0, **kw):
        op("g", [], [o], lambda: g.iota(ap(o), pat, 0, cm, **kw))

    def asel(o, i, pat, f, base, cm):
        op("g", [i], [o], lambda: g.affine_select(ap(o), ap(i), pat, f, 0.0, base, cm))

    def dma(q, o, i, rd, wr, sem):
        hold(q, rd, wr)
        ENG[q].dma_start(o, i).then_inc(T.sem[sem], 16)
        done(q, rd, wr, (sem, 16))

    def send(to, rsem, *pairs):
        c = T.cores[to % 8]
        adr, ne = topo.addr(c), len(topo.engines(core, c))
        for dst, src in pairs:
            hold("g", [src], [])
            CNT["ls"] += ne
            g.remote_dma(ap(dst), ap(src), T.sem[rsem], T.sem["ls"], adr[1], adr[0], topo.mask(core, c))
        seq[0] += 1
        ev = (rsem, ne * len(pairs))
        clocks[ev] = {ev[0]: ev[1], "#": seq[0]}
        for r, src in pairs:
            writes.setdefault(r[0], []).append((r[1:4], ev, "far"))

    dma("s", ap(R("xt0")), T.x[:, :], [], [R("xt0")], "dx")
    dma("a", ap(R("ut")), T.u[:, :], [], [R("ut")], "du")
    dma("a", ap(R("li")), T.link[:, :], [], [R("li")], "dl")
    dma("s", ap(R("wq", bit="u8")), T.wc[:, :], [], [R("wq")], "dw")
    dma("s", ap(R("wqs")), T.ws[:, :], [], [R("wqs")], "ds")
    dma("s", ap(R("vt")), T.v[:, :], [], [R("vt")], "dv")

    KCB, JB, UO = R("kj", 0, 24), R("kj", 24, 36), R("pi", 4, 12)
    fine = {"allow_small_or_imprecise_dtypes": True}
    iota(R("pi", 0, 1), [[1, 1]], 1)
    iota(R("ks"), [[1, 16]], **fine)
    iota(UO, [[16, 8]])
    iota(KCB, [[16, 24]], **fine)
    iota(JB, [[16, 12]], **fine)
    iota(R("ks4"), [[0, 4], [1, 4]], **fine)
    iota(R("iota0"), [[1, 384]], **fine)
    iota(R("alt"), [[0, 192], [1024, 2]], **fine)

    col = {n: R("cols", i, i + 1) for i, n in enumerate(("pm", "pm1", "p4", "p41", "b16", "b4", "bb", "thr", "k2", "pb4", "pbn", "z"))}
    fill(R("one"), 1.0)
    ts(R("pi", 1, 2), R("pi", 0, 1), 15, AL.bitwise_and)
    ts(R("pi", 2, 3), R("pi", 0, 1), 2, AL.logical_shift_right, 3, AL.bitwise_and)
    ts(R("pi", 3, 4), R("pi", 0, 1), 3, AL.bitwise_and)
    fill(R("ow", 0, 24), 0.0)
    cp(col["pm"], R("pi", 1, 2))
    cp(col["p4"], R("pi", 2, 3))
    ts(col["pm1"], R("pi", 1, 2), 1.0, AL.add)
    ts(col["p41"], R("pi", 2, 3), 1.0, AL.add)
    ts(col["b16"], col["pm"], 14.5, AL.is_lt, BV, AL.mult)
    ts(col["b4"], col["p4"], 2.5, AL.is_lt, BV, AL.mult)
    ts(R("pmo"), R("ow", 0, 24), col["pm"], AL.add)
    for b in range(4):
        act(R("iet", 512 * b, 512 * b + 512), R("one"), scale=0.0)
    asel(R("bot"), R("one"), [[-16, 8], [0, 64]], AL.is_ge, 0, 1)
    asel(R("bot"), R("bot"), [[16, 8], [0, 64]], AL.is_ge, 15, -1)
    for b in range(4):
        asel(R("iet", 512 * b + b, 512 * b + 512, 4), R("one", 0, 128), [[-1, 128]], AL.is_equal, 0, 1)
    ts(R("ta"), R("ks"), col["pm"], AL.is_equal, 2 * BIG, AL.mult)
    ts(R("rsw"), R("ks"), 0.5, AL.is_gt, 2 * BIG, AL.mult)
    ts(R("r0w"), R("ks"), 0.5, AL.is_gt)
    ts(R("mbw"), R("ta"), -BIG, AL.add)
    ts(R("rsw"), R("rsw"), -BIG, AL.add)
    act(R("mb"), IND(R("mbw"), R("pmo")))
    act(R("rs"), IND(R("rsw"), R("pmo")))
    ts(R("ta"), R("ks"), col["pm"], AL.is_equal, -2 * BV, AL.mult)
    ts(R("tn"), R("ks"), col["pm1"], AL.is_equal, BV, AL.mult)
    ts(R("t16w"), R("ks"), 0.5, AL.is_lt, -8 * BV, AL.mult)
    tt(R("ta"), R("ta"), R("tn"), AL.add)
    ts(R("uo16", 0, 8), UO, 0.0, AL.add)
    ts(R("uo16", 8, 16), UO, 1.0, AL.add)
    tt(R("t16w"), R("t16w"), R("ta"), AL.add)
    ts(col["bb"], col["b16"], 2.0 ** -18, AL.mult)
    ts(col["thr"], col["b16"], 2.0 ** -18, AL.mult, 0.5, AL.add)
    ts(R("tbw"), R("t16w"), 2.0 ** -18, AL.mult)
    act(R("tb"), IND(R("tbw"), R("pmo")))
    act(R("r0"), IND(R("r0w"), R("pmo")))
    act(R("t16"), IND(R("t16w"), R("pmo")))
    for n, ls, w in TILES[:2]:
        fill(R(n, 64 * ls[-1], 4 * w), 0.0)
    fill(R("ru", 0, 1), 0.0)
    quant("uq", R("ut"))
    for n, lo in (("urs", 0), ("urb", 8)):
        cp(R(n, bit="u32"), IND(R("uq", bit="u32"), R("uo16", lo, lo + 8)))
        cp(R(n + "s"), IND(R("uqs"), R("uo16", lo, lo + 8)))
    fill(R("zt"), 0.0)
    fill(R("ak", 384, 512), 0.0)
    fill(R("al", 384, 512), 0.0)

    xin = "xt0"
    for t in range(NR):
        d = 2 ** t
        xn, lr, qk, vb = "xt%d" % (t + 1), "lr%d" % t, "qk%d" % t, "vb%d" % t
        sb, lb, sn, ln, st, lt = ["%s%d" % (n, t) for n in ("sb", "lb", "sn", "ln", "st", "lt")]
        P = [R("p%d" % b, 0, 384) for b in range(8)]
        quant("xq", R(xin))
        mm(P[0], "urs", 0, "xq", 384)
        mm(P[1], "urb", 0, "xq", 384)
        mm(P[7], "urs", 0, "xq", 384)
        if t:
            for b in range(4):
                mm(P[2 + b], "eq", 128 * b, "xq", 384)
            scan(R("lc"), R("t16"), R(lr))
        else:
            for k in range(NR):
                quant("vb%d" % k, R("zt"))
        act(R("sg"), P[1], AF.Sign)
        tt(R("m2"), P[0], R("mb"), AL.min)
        if t:
            ts(R("ow", 48, 72), R("lc", 15, 384, 16), col["b16"], AL.subtract)
            ts(R("lt16"), R("lc", 15, 384, 16), col["b16"], AL.subtract)
        else:
            cp(R("lt16"), R("li"))
            cp(R("ow", 48, 72), R("li"))
        scan(R("hs"), R("rs"), R("m2"), AL.min)
        scan(R("bt"), R("tb"), R("sg"))
        tt(R("fa", 3, 1536, 4), P[0], R("hs"), AL.is_le)
        ts(R(sb), R("bt", 15, 384, 16), col["thr"], AL.is_gt)
        send(rank - d, "rb%d" % t, (R(lb), R(sb)))
        for n, ls, w in TILES[2:] if t == 0 else []:
            iota(R(n, 64 * ls[-1], 4 * w), [[0, 4 * w - 64 * ls[-1]]], **fine)
        if t:
            for b in range(2):
                act(R(xn, b, 1536, 4), P[2 + b])
        for k, c in enumerate((23, 22, 21)):
            act(R("sgl", 368 * k, 368 * k + 16 * c), R("p7", 0, 16 * c), AF.Sign, scale=-1.0, bias=R("hs", 16 * c + 15, 16 * c + 16))
        ju = [0]

        def layer(fn, k, c, by=None):
            n = 16 * c
            if by is None:
                ts(R(fn, k, 4 * n, 4), R("p0", 0, n), R("hs", n + 15, n + 16), AL.is_lt)
            else:
                ts(R(fn, k, 4 * n, 4), R("sgl", 368 * by, 368 * by + n), 0.5, AL.is_gt)
            act(R("junk", ju[0], ju[0] + n), R(fn, k, 4 * n, 4), accum=R("ru", c, c + 1))
            ju[0] += n

        for k in range(4):
            layer("fb", k, 20 - k)
        for k in range(3):
            layer("fa", k, 23 - k, k)
        for ti, (fn, ls, w) in enumerate(TILES):
            todo = [(TILES[ti + 1][0], k, c) for k, c in enumerate(TILES[ti + 1][1]) if c < 17] if ti < 5 else []
            for x in todo[:1]:
                layer(*x)
            if ti == 0:
                if t == 0:
                    act(R(lr), IND(R("iota0"), R("lt16")))
                    quant("bo", R("bot"))
                    ts(KCB, KCB, 15.0, AL.add, col["pm"], AL.subtract)
                    ts(JB, JB, col["pm"], AL.add, col["b16"], AL.add)
                    ts(col["k2"], col["b16"], -1.0, AL.mult, 191.0, AL.add)
                    ts(KCB, KCB, col["b16"], AL.subtract)
                scan(R("rds"), R("r0"), R("fa", 3, 1536, 4), AL.mult, AL.add)
            if ti == 5:
                cp(R("off16"), R("ow", 24, 48))
            quant("q" + fn, R(fn))
            mm(R("p6", 0, w), "bo", 0, "q" + fn, w, start=ti == 0, stop=ti == 5)
            if ti == 0:
                tt(R("kr", 0, 24), KCB, R("rds", 15, 384, 16), AL.subtract)
                if t == 0:
                    ts(R("ta"), R("ks4"), col["p4"], AL.is_equal, -2 * BV, AL.mult)
                    ts(R("tn"), R("ks4"), col["p41"], AL.is_equal, BV, AL.mult)
                    ts(R("t4w"), R("ks4"), 0.5, AL.is_lt, -8 * BV, AL.mult)
                    tt(R("ta"), R("ta"), R("tn"), AL.add)
                    cp(col["pb4"], R("pi", 3, 4))
                    ts(col["z"], col["b4"], -4.0, AL.mult)
                    tt(R("t4w"), R("t4w"), R("ta"), AL.add)
                    tt(col["pbn"], col["z"], col["pb4"], AL.add)
                    ts(R("cw"), R("ks"), 512.0, AL.mult)
                    ts(R("cv"), R("ks"), -512.0, AL.mult, 512.0, AL.add)
                    act(R("t4"), IND(R("t4w"), R("pmo", 0, 12)))
            if ti == 2:
                act(R("w2", 0, 384), IND(R("cw"), R(lb)))
                act(R("w2", 384, 768), IND(R("cv"), R(lb)))
                ts(R("ow", 0, 24), R("bt", 15, 384, 16), col["thr"], AL.is_gt, 384.0, AL.mult)
            if ti == 3:
                tt(R("ow", 24, 48), R("ow", 0, 24), R("ow", 48, 72), AL.add)
            for x in todo[1:]:
                layer(*x)
        if t == 0:
            quant("eq", R("iet"))
            for b in range(4):
                mm(P[2 + b], "eq", 128 * b, "xq", 384)
        tt(R("pay"), IND(R("w2"), R("off16")), R("iota0"), AL.add)
        scan(R("mc"), R("t16"), P[6])
        tt(R("kr", 24, 48), R("kr", 0, 24), R("ru"), AL.subtract)
        tt(R("kr", 48, 72), R("mc", 15, 384, 16), R("kr", 24, 48), AL.add)
        cp(R("rk16"), R("kr", 48, 72))
        cp(IND(R("sp"), R("rk16")), R("pay"))
        for b in range(2 if t else 0, 4):
            act(R(xn, b, 1536, 4), P[2 + b])
        act(R("fh"), R(xn), scale=0.5)

        def pairs(a, b):
            scan(R("kq", a, b), R("alt", a, b), R("sp", a, b), AL.mult, AL.add)

        flt, pp1, pp2, pp3, nn = [R("pp", 12 * i, 12 * i + 12) for i in range(5)]
        ts(R("fl"), R("sp", 1, 384, 2), 511.5, AL.is_gt)
        pairs(0, 128)
        scan(R("fcum"), R("fl"), R("fl"))
        scan(R("flc"), R("tb", 0, 192), R("fl"))
        scan(R("fc2"), R("t16", 0, 192), R("fcum"))
        ts(flt, R("flc", 15, 192, 16), col["bb"], AL.subtract)
        ts(pp2, R("fc2", 15, 192, 16), R("fcum", 191, 192), AL.subtract, col["k2"], AL.add)
        tt(pp1, JB, R("fc2", 15, 192, 16), AL.subtract)
        tt(pp3, pp2, flt, AL.mult)
        pairs(128, 256)
        tt(nn, pp1, pp3, AL.max)
        pairs(256, 384)
        cp(R("n16"), nn)
        cp(IND(R("kqs"), R("n16")), R("kq", 1, 384, 2))
        scan(R("c4"), R("t4"), R("kqs"))
        scan(R("c16"), R("t16", 0, 192), R("kqs"))
        ts(R("kqi", 0, 48), R("c4", 3, 192, 4), col["b4"], AL.subtract)
        ts(R("kqi", 48, 60), R("c16", 15, 192, 16), col["b16"], AL.subtract)
        ts(R("kqi", 60, 108), R("kqi", 0, 48), 511, AL.bitwise_and)
        ts(R("kqi", 120, 168), R("kqi", 0, 48), 10, AL.logical_shift_right, 511, AL.bitwise_and)
        ts(R("t4q"), R("kqi", 60, 108), 4.0, AL.mult, col["pb4"], AL.add)
        ts(R("kqi", 108, 120), R("kqi", 48, 60), 511, AL.bitwise_and)
        ts(R("t4k"), R("kqi", 120, 168), 4.0, AL.mult, col["pb4"], AL.add)
        cp(R("tqk"), R("kqi", 108, 114))
        ts(R("kqi", 168, 180), R("kqi", 48, 60), 10, AL.logical_shift_right, 511, AL.bitwise_and)
        act(R("fq", 0, 192), IND(R("fh"), R("t4q", 0, 12)))
        act(R("fq", 192, 384), IND(R("fh"), R("t4q", 12, 24)))
        act(R("fq", 384, 768), IND(R("fh"), R("t4q", 24, 48)))
        cp(R("lqk"), IND(R(lr), R("tqk")))
        tt(R("ak", 0, 192), IND(R("fh"), R("t4k", 0, 12)), R("fq", 0, 192), AL.add)
        scan(R("nmc"), R("t4", 0, 96), R("lqk"))
        cp(R("tll", 0, 6), R("kqi", 114, 120))
        ts(R(sn), R("nmc", 3, 96, 4), 4.0, AL.mult, col["pbn"], AL.add)
        send(rank + d, "rn%d" % t, (R(ln), R(sn)))
        tt(R("ak", 192, 384), IND(R("fh"), R("t4k", 12, 24)), R("fq", 192, 384), AL.add)
        cp(R("tll", 6, 12), R("kqi", 174, 180))
        quant(qk, R("ak"))
        send(rank + d, "rc%d" % t, (R(vb, 0, 96, 1, "u8"), R(qk, 0, 96, 1, "u8")), (R(vb + "s", 0, 96), R(qk + "s", 0, 96)))
        tt(R("al", 0, 384), IND(R("fh"), R("t4k", 24, 48)), R("fq", 384, 768), AL.add)
        quant("ql", R("al"))
        act(R("val", 0, 96), IND(R(lr), R("tll", 6, 12)))
        act(R("val", 96, 192), IND(R(lr), R("tll", 0, 6)))
        act(R("tu"), R(lr))
        act(R("fl32"), R("fq", 384, 768), scale=64.0)
        left = ("p0", "p1", "p6", "p7")
        for b in range(4):
            mm(R(left[b], 0, 128), "wq", 128 * b, "ql", 128)
        cp(IND(R("tu"), R("tll")), R("val"))
        for b in range(4):
            tt(R("sl", b, 384, 4), R(left[b], 0, 96), R("fl32", b, 384, 4), AL.add)
        act(R("rl"), R("sl"), scale=0.03125)
        scan(R("tuc"), R("t16"), R("tu"))
        if t == 0:
            quant("vq", R("vt"))
        ts(R(st), R("tuc", 15, 384, 16), col["b16"], AL.subtract)
        send(rank - d, "rt%d" % t, (R(lt), R(st)))
        cp(IND(R(xn), R("t4q", 24, 48)), R("rl"))
        act(R("fn32"), IND(R("fh"), R(ln)), scale=64.0)
        for b in range(4):
            mm(R("p%d" % (2 + b), 0, 128), "wq", 128 * b, vb, 128)
        for b in range(4):
            tt(R("sa", b, 384, 4), R("p%d" % (2 + b), 0, 96), R("fn32", b, 384, 4), AL.add)
            act(R("ra", b, 384, 4), R("sa", b, 384, 4), scale=0.03125)
        act(R("tr"), IND(R("iota0"), R(lt)))
        act(R("lr%d" % (t + 1)), IND(R("tr"), R("lt16")))
        cp(IND(R(xn), R(ln)), R("ra"))
        xin = xn
    quant("xq", R(xin))
    for b in range(2):
        mm(R("p%d" % b, 0, 192), "vq", 0, "xq", 192, lo=192 * b)
    dma("s", T.oc[:, :], ap(R("xq", bit="u8")), [R("xq")], [], "oc_")
    for k in range(4):
        dma("s", T.osc[4 * k:4 * k + 4, :], T.xqs[32 * k:32 * k + 4, 0:384], [R("xqs")], [], "o%d" % k)
    dma("s", T.lk[:, :], T.lr3[0:128:16, :], [R("lr3")], [], "ok")
    act(R("ys", 0, 192), R("p0", 0, 192))
    dma("a", T.y[:, 0:192], ap(R("ys", 0, 192)), [R("ys", 0, 192)], [], "oy")
    cp(R("ys", 192, 384), R("p1", 0, 192))
    dma("s", T.y[:, 192:384], ap(R("ys", 192, 384)), [R("ys", 192, 384)], [], "oz")
    for s in ("oc_", "o0", "o1", "o2", "o3", "oy", "oz", "ok"):
        g.wait_ge(T.sem[s], 16)
    for s in ("v", "a", "p", "gc", "ls"):
        g.wait_ge(T.sem[s], CNT[s])
